import numpy as np
import ml_dtypes


def mxq(x, axis, fmt="e4m3"):
    dtype, down = {"e4m3": (ml_dtypes.float8_e4m3fn, 7), "e5m2": (ml_dtypes.float8_e5m2, 14)}[fmt]
    v = np.moveaxis(np.asarray(x, np.float32).astype(ml_dtypes.bfloat16).astype(np.float64), axis, -1)
    blocks = v.reshape(v.shape[:-1] + (-1, 32))
    amax = np.abs(blocks).max(-1, keepdims=True)
    byte = np.maximum(np.where(amax > 0, np.frexp(amax)[1] - 1 + 127, 0) - down, 1)
    scale = np.exp2(byte - 127.0)
    codes = (blocks / scale).astype(np.float32).astype(dtype).astype(np.float64)
    return np.moveaxis((codes * scale).reshape(v.shape), -1, axis)


WIDE = False


def mx_kscale(k):
    if not WIDE:
        return np.ones(k)
    levels = np.array([10, -10, 5, -5, 0])
    if k % 512:
        return np.exp2(np.random.permutation(np.resize(levels, k // 32))).repeat(32)
    a = np.empty((k // 512, 16))
    for p in range(k // 512):
        a[p, :8] = np.random.permutation(np.resize(levels, 8))
        for g in range(8):
            far = levels[np.abs(levels - a[p, g]) >= 10]
            a[p, g + 8] = far[np.random.randint(len(far))]
    return np.exp2(a.ravel()).repeat(32)


def f64(x):
    return np.asarray(x).astype(np.float64)


def striped(idx):
    return np.tile(np.asarray(idx).reshape(-1, 16).T, (8, 1)).astype(np.uint16)


def unstriped(offs):
    return offs[:16].T.reshape(-1).astype(np.int64)


E2M1 = np.array([0.0, 0.5, 1.0, 1.5, 2.0, 3.0, 4.0, 6.0, -0.0, -0.5, -1.0, -1.5, -2.0, -3.0, -4.0, -6.0])


def pack_weight(w, fmt):
    k, n = w.shape
    w = f64(np.asarray(w, np.float32).astype(ml_dtypes.bfloat16)).reshape(k // 32, 32, n)
    amax = np.abs(w).max(1)
    if fmt == "e4m3":
        byte = np.frexp(amax)[1] - 1 + 127 - 7
    else:
        mant, ex = np.frexp(amax / 6.0)
        byte = np.where(mant > 0.5, ex, ex - 1) + 127
    byte = np.clip(np.where(amax > 0, byte, 1), 1, 254)
    scaled = (w * np.exp2(127.0 - byte)[:, None, :]).reshape(k, n).astype(np.float32)
    by_word = np.ascontiguousarray(scaled.reshape(k // 512, 128, 4, n).transpose(0, 1, 3, 2))
    if fmt == "e4m3":
        words = by_word.astype(ml_dtypes.float8_e4m3fn).view(np.uint8)
    else:
        c = by_word.astype(ml_dtypes.float4_e2m1fn).view(np.uint8) & 0xF
        words = (c[..., 0::2] | (c[..., 1::2] << 4)).reshape(k // 512, 128, 2 * n)
    return np.ascontiguousarray(words), np.ascontiguousarray(byte.astype(np.uint8).reshape(k // 512, 16, n))


def unpack_weight(words, scales, fmt):
    g, _, n = scales.shape
    words = np.ascontiguousarray(words).reshape(g, 128, n, -1)
    if fmt == "e4m3":
        vals = words.view(ml_dtypes.float8_e4m3fn).astype(np.float64)
    else:
        nib = np.empty((g, 128, n, 4), np.uint8)
        nib[..., 0::2] = words & 0xF
        nib[..., 1::2] = words >> 4
        vals = E2M1[nib]
    vals = vals * np.repeat(np.exp2(scales.astype(np.float64) - 127.0), 8, axis=1)[..., None]
    return vals.transpose(0, 1, 3, 2).reshape(g * 512, n)


def bf(x):
    return np.asarray(x, np.float32).astype(ml_dtypes.bfloat16)


def planes(Y):
    r, m = Y.shape
    b = f64(bf(Y)).reshape(r // 32, 32, m)
    amax = np.abs(b).max(1)
    byte = np.clip(np.where(amax > 0, np.frexp(amax)[1] - 1 + 127 - 7, 1), 1, 254)
    codes = (b * np.exp2(127.0 - byte)[:, None, :]).reshape(r, m).astype(np.float32).astype(ml_dtypes.float8_e4m3fn).view(np.uint8)
    words = codes.reshape(r // 512, 128, 4, m).transpose(0, 1, 3, 2)
    return np.ascontiguousarray(words), np.ascontiguousarray(byte.astype(np.uint8).reshape(r // 512, 16, m))


B, N, T, D, NQ = 1, 512, 2048, 512, 512


def setup_inputs():
    n = np.random.standard_normal
    idx = np.random.permutation(T)[:B * N]
    s = mx_kscale(D)[:, None]
    kp = pack_weight(n((D, T)) / s, "e4m3")
    cp = pack_weight(n((D, T)) / s, "e4m3")
    return {
        "qT": (n((B, D, NQ)) * s * (1.00 / np.sqrt(D))).astype(np.float32),
        "k_words": kp[0],
        "k_scales": kp[1],
        "c_words": cp[0],
        "c_scales": cp[1],
        "offs": striped(idx),
    }


def reference(qT, k_words, k_scales, c_words, c_scales, offs):
    idx = unstriped(offs)
    pick = lambda x, which: x[:, which].reshape(x.shape[0], B, -1).transpose(1, 0, 2)
    k = unpack_weight(k_words, k_scales, "e4m3")
    kg = pick(k, idx)
    c = unpack_weight(c_words, c_scales, "e4m3")
    cg = pick(c, idx)
    qq = mxq(f64(qT), 1, "e4m3")
    a = qq.transpose(0, 2, 1) @ kg
    z = qq.transpose(0, 2, 1) @ cg
    g = a - 0.5 * z
    m = np.max(g, axis=-1, keepdims=True)
    e = np.exp(g - m)
    y = e / np.sum(e, axis=-1, keepdims=True)
    Y = y[0]
    words, scales = planes(Y)
    return Y, words, scales

@@ -1,0 +1,166 @@
+from contextlib import ExitStack
+
+import concourse.mybir as mybir
+
+F32 = mybir.dt.float32
+BF16 = mybir.dt.bfloat16
+I32 = mybir.dt.int32
+U32 = mybir.dt.uint32
+U16 = mybir.dt.uint16
+U8 = mybir.dt.uint8
+FP8X4 = mybir.dt.float8_e4m3fn_x4
+ALU = mybir.AluOpType
+ACT = mybir.ActivationFunctionType
+AX = mybir.AxisListType
+
+P = 128
+PACK = 4
+T = 2048
+N = 512
+NQ = 512
+D = 512
+C_ROW = 8
+V_COLS = 384
+
+FLOPS = 2 * 2 * NQ * N * D
+
+
+def tile_attend_plq_contrast_topk_kernel(tc, qT, k_words, k_scales, c_words, c_scales, offs, out_0, out_1, out_2):
+    nc = tc.nc
+    with ExitStack() as ctx:
+        keep = ctx.enter_context(tc.tile_pool(name="keep", bufs=1))
+        psum = ctx.enter_context(tc.psum_pool(name="psum", bufs=1))
+
+        offsets = keep.tile([P, N // 16], U16, name="offsets")
+        q_raw = keep.tile([P, PACK, NQ], F32, name="q_raw")
+        kw = keep.tile([P, T], I32, name="kw", align_bytes=64)
+        cw = keep.tile([P, T], I32, name="cw", align_bytes=64)
+        ks = keep.tile([P, T], U8, name="ks", align_bytes=64)
+        cs = keep.tile([P, T], U8, name="cs", align_bytes=64)
+
+        nc.vector.memset(cs[:].bitcast(I32), 0)
+        nc.gpsimd.memset(ks[:].bitcast(I32), 0)
+
+        nc.sync.dma_start(out=q_raw[:], in_=qT[0].rearrange("(p j) q -> p j q", j=PACK))
+        nc.sync.dma_start(offsets[:], offs)
+        for r in range(4):
+            nc.scalar.dma_start(out=cs[C_ROW + r : P : 32, :].bitcast(I32), in_=c_scales[0, r:16:4, :].bitcast(I32))
+        nc.sync.dma_start(out=cw[:], in_=c_words[0].rearrange("p t r -> p (t r)").bitcast(I32))
+        nc.sync.dma_start(out=kw[:], in_=k_words[0].rearrange("p t r -> p (t r)").bitcast(I32))
+        for r in range(4):
+            nc.gpsimd.dma_start(out=ks[r:P:32, :].bitcast(I32), in_=k_scales[0, r:16:4, :].bitcast(I32))
+
+        csg = keep.tile([P, N], U8, name="csg", align_bytes=64)
+        ksg = keep.tile([P, N], U8, name="ksg", align_bytes=64)
+        cwg = keep.tile([P, N], U32, name="cwg", align_bytes=64)
+        kwg = keep.tile([P, N], U32, name="kwg", align_bytes=64)
+
+        nc.vector.tensor_copy(csg[:], cs[:].indirect(offsets[:]))
+
+        q_bf = keep.tile([P, PACK, P, PACK], BF16, name="q_bf", align_bytes=64)
+        nc.scalar.activation(
+            out=q_bf[:].rearrange("p r m j -> p m j r"),
+            in_=q_raw[:].rearrange("p j (m r) -> p m j r", r=PACK),
+            func=ACT.Copy,
+        )
+        q_codes = keep.tile([P, NQ], U32, name="q_codes", align_bytes=64)
+        q_scales = keep.tile([P, NQ], U8, name="q_scales", align_bytes=64)
+        nc.vector.quantize_mx(
+            out=q_codes[:].bitcast(FP8X4), scales=q_scales[:], in_=q_bf[:].rearrange("p r m j -> p (r m j)")
+        )
+
+        nc.vector.tensor_copy(cwg[:], cw[:].bitcast(U32).indirect(offsets[:]))
+        nc.vector.tensor_copy(ksg[:], ks[:].indirect(offsets[:]))
+
+        z_sb = []
+        for r in range(PACK):
+            cols = slice(r * P, (r + 1) * P)
+            z_ps = psum.tile([P, N], F32, name=f"z_ps{r}")
+            nc.tensor.matmul_mx(
+                out=z_ps[:], lhsT=q_codes[:, cols].bitcast(FP8X4), lhsT_scale=q_scales[:, cols],
+                rhs=cwg[:].bitcast(FP8X4), rhs_scale=csg[C_ROW:P, :], start=True, stop=True,
+            )
+            half_z = keep.tile([P, N], F32, name=f"half_z{r}")
+            nc.scalar.activation(out=half_z[:], in_=z_ps[:], func=ACT.Copy, scale=-0.5)
+            z_sb.append(half_z)
+
+        nc.vector.tensor_copy(kwg[:], kw[:].bitcast(U32).indirect(offsets[:]))
+
+        y = keep.tile([P, PACK, N], F32, name="y")
+        out_rows = out_0.rearrange("(p r) i -> p r i", r=PACK)
+        g_tiles, e_tiles, sums = [], [], []
+
+        def scores(r):
+            cols = slice(r * P, (r + 1) * P)
+            a_ps = psum.tile([P, N], F32, name=f"a_ps{r}")
+            nc.tensor.matmul_mx(
+                out=a_ps[:], lhsT=q_codes[:, cols].bitcast(FP8X4), lhsT_scale=q_scales[:, cols],
+                rhs=kwg[:].bitcast(FP8X4), rhs_scale=ksg[:], start=True, stop=True,
+            )
+            g = keep.tile([P, N], F32, name=f"g{r}")
+            nc.vector.tensor_tensor(out=g[:], in0=a_ps[:], in1=z_sb[r][:], op=ALU.add)
+            g_tiles.append(g)
+
+        def weights(r):
+            g = g_tiles[r]
+            neg_max = keep.tile([P, 1], F32, name=f"neg_max{r}")
+            nc.vector.tensor_reduce(out=neg_max[:], in_=g[:], axis=AX.X, op=ALU.max, negate=True)
+            e = keep.tile([P, N], F32, name=f"e{r}")
+            total = keep.tile([P, 1], F32, name=f"total{r}")
+            nc.scalar.activation(out=e[:], in_=g[:], func=ACT.Exp, bias=neg_max[:], accum_out=total[:])
+            e_tiles.append(e)
+            sums.append(total)
+
+        def inverse(r):
+            inv = keep.tile([P, 1], F32, name=f"inv{r}")
+            nc.vector.reciprocal(out=inv[:], in_=sums[r][:])
+            return inv
+
+        def norm_scalar(r, inv, lo, hi):
+            nc.scalar.activation(out=y[:, r, lo:hi], in_=e_tiles[r][:, lo:hi], func=ACT.Copy, scale=inv[:])
+
+        def norm_vector(r, inv, lo, hi):
+            nc.vector.tensor_scalar(out=y[:, r, lo:hi], in0=e_tiles[r][:, lo:hi], scalar1=inv[:], scalar2=None, op0=ALU.mult)
+
+        scores(0)
+        scores(1)
+        weights(0)
+        scores(2)
+        weights(1)
+        norm_scalar(0, inverse(0), 0, N)
+        nc.sync.dma_start(out=out_rows[:, 0, :], in_=y[:, 0, :])
+        scores(3)
+        weights(2)
+        weights(3)
+        norm_vector(1, inverse(1), 0, N)
+        nc.sync.dma_start(out=out_rows[:, 1, :], in_=y[:, 1, :])
+        norm_vector(2, inverse(2), 0, N)
+        nc.sync.dma_start(out=out_rows[:, 2, :], in_=y[:, 2, :])
+        inv3 = inverse(3)
+        norm_vector(3, inv3, 0, V_COLS)
+        norm_scalar(3, inv3, V_COLS, N)
+        nc.sync.dma_start(out=out_rows[:, 3, :], in_=y[:, 3, :])
+
+        y_bf = keep.tile([P, N, PACK], BF16, name="y_bf", align_bytes=64)
+        dst = y_bf[:].rearrange("p (c i) r -> p c r i", i=4)
+        src = y[:].rearrange("p r (c i) -> p c r i", i=4)
+        nc.vector.tensor_copy(out=dst[:, : V_COLS // 4], in_=src[:, : V_COLS // 4])
+        nc.scalar.copy(out=dst[:, V_COLS // 4 :], in_=src[:, V_COLS // 4 :])
+
+        y_codes = keep.tile([P, N], U32, name="y_codes", align_bytes=64)
+        y_scales = keep.tile([P, N], U8, name="y_scales", align_bytes=64)
+        words_out = out_1[0].rearrange("p i u -> p (i u)").bitcast(I32)
+        flat = y_bf[:].rearrange("p i r -> p (i r)")
+        for lo, hi in ((0, 256), (256, 512)):
+            cols = slice(lo, hi)
+            nc.vector.quantize_mx(
+                out=y_codes[:, cols].bitcast(FP8X4), scales=y_scales[:, cols],
+                in_=flat[:, PACK * lo : PACK * hi],
+            )
+            nc.sync.dma_start(out=words_out[:, cols], in_=y_codes[:, cols].bitcast(I32))
+        for quad in range(4):
+            queue = nc.scalar if quad % 2 else nc.sync
+            queue.dma_start(
+                out=out_2[0, 4 * quad : 4 * quad + 4, :].bitcast(I32),
+                in_=y_scales[32 * quad : 32 * quad + 4, :].bitcast(I32),
+            )

@@ -20,7 +20,9 @@ N = 512
 NQ = 512
 D = 512
 C_ROW = 8
-V_COLS = 384
+V_COLS = 304
+G_COLS = (0, 0, 512, 256)
+Q_SPLIT = 96
 
 FLOPS = 2 * 2 * NQ * N * D
 
@@ -39,16 +41,16 @@ def tile_attend_plq_contrast_topk_kernel(tc, qT, k_words, k_scales, c_words, c_s
         cs = keep.tile([P, T], U8, name="cs", align_bytes=64)
 
         nc.vector.memset(cs[:].bitcast(I32), 0)
-        nc.gpsimd.memset(ks[:].bitcast(I32), 0)
+        nc.vector.memset(ks[:].bitcast(I32), 0)
 
         nc.sync.dma_start(out=q_raw[:], in_=qT[0].rearrange("(p j) q -> p j q", j=PACK))
+        for r in range(4):
+            nc.sync.dma_start(out=cs[C_ROW + r : P : 32, :].bitcast(I32), in_=c_scales[0, r:16:4, :].bitcast(I32))
         nc.sync.dma_start(offsets[:], offs)
-        for r in range(4):
-            nc.scalar.dma_start(out=cs[C_ROW + r : P : 32, :].bitcast(I32), in_=c_scales[0, r:16:4, :].bitcast(I32))
         nc.sync.dma_start(out=cw[:], in_=c_words[0].rearrange("p t r -> p (t r)").bitcast(I32))
-        nc.sync.dma_start(out=kw[:], in_=k_words[0].rearrange("p t r -> p (t r)").bitcast(I32))
         for r in range(4):
-            nc.gpsimd.dma_start(out=ks[r:P:32, :].bitcast(I32), in_=k_scales[0, r:16:4, :].bitcast(I32))
+            nc.sync.dma_start(out=ks[r:P:32, :].bitcast(I32), in_=k_scales[0, r:16:4, :].bitcast(I32))
+        nc.sync.dma_start(out=kw[:], in_=k_words[0].rearrange("p t r -> p (t r)").bitcast(I32))
 
         csg = keep.tile([P, N], U8, name="csg", align_bytes=64)
         ksg = keep.tile([P, N], U8, name="ksg", align_bytes=64)
@@ -58,11 +60,10 @@ def tile_attend_plq_contrast_topk_kernel(tc, qT, k_words, k_scales, c_words, c_s
         nc.vector.tensor_copy(csg[:], cs[:].indirect(offsets[:]))
 
         q_bf = keep.tile([P, PACK, P, PACK], BF16, name="q_bf", align_bytes=64)
-        nc.scalar.activation(
-            out=q_bf[:].rearrange("p r m j -> p m j r"),
-            in_=q_raw[:].rearrange("p j (m r) -> p m j r", r=PACK),
-            func=ACT.Copy,
-        )
+        q_dst = q_bf[:].rearrange("p r m j -> p m j r")
+        q_src = q_raw[:].rearrange("p j (m r) -> p m j r", r=PACK)
+        nc.scalar.activation(out=q_dst[:, :Q_SPLIT], in_=q_src[:, :Q_SPLIT], func=ACT.Copy)
+        nc.vector.tensor_copy(out=q_dst[:, Q_SPLIT:], in_=q_src[:, Q_SPLIT:])
         q_codes = keep.tile([P, NQ], U32, name="q_codes", align_bytes=64)
         q_scales = keep.tile([P, NQ], U8, name="q_scales", align_bytes=64)
         nc.vector.quantize_mx(
@@ -88,7 +89,7 @@ def tile_attend_plq_contrast_topk_kernel(tc, qT, k_words, k_scales, c_words, c_s
 
         y = keep.tile([P, PACK, N], F32, name="y")
         out_rows = out_0.rearrange("(p r) i -> p r i", r=PACK)
-        g_tiles, e_tiles, sums = [], [], []
+        g_tiles, e_tiles, sums = {}, [], []
 
         def scores(r):
             cols = slice(r * P, (r + 1) * P)
@@ -98,8 +99,14 @@ def tile_attend_plq_contrast_topk_kernel(tc, qT, k_words, k_scales, c_words, c_s
                 rhs=kwg[:].bitcast(FP8X4), rhs_scale=ksg[:], start=True, stop=True,
             )
             g = keep.tile([P, N], F32, name=f"g{r}")
-            nc.vector.tensor_tensor(out=g[:], in0=a_ps[:], in1=z_sb[r][:], op=ALU.add)
-            g_tiles.append(g)
+            n_g = G_COLS[r]
+            if n_g:
+                a_sb = keep.tile([P, n_g], F32, name=f"a_sb{r}")
+                nc.scalar.copy(out=a_sb[:], in_=a_ps[:, :n_g])
+                nc.gpsimd.tensor_tensor(out=g[:, :n_g], in0=a_sb[:], in1=z_sb[r][:, :n_g], op=ALU.add)
+            if n_g < N:
+                nc.vector.tensor_tensor(out=g[:, n_g:], in0=a_ps[:, n_g:], in1=z_sb[r][:, n_g:], op=ALU.add)
+            g_tiles[r] = g
 
         def weights(r):
             g = g_tiles[r]
@@ -122,18 +129,20 @@ def tile_attend_plq_contrast_topk_kernel(tc, qT, k_words, k_scales, c_words, c_s
         def norm_vector(r, inv, lo, hi):
             nc.vector.tensor_scalar(out=y[:, r, lo:hi], in0=e_tiles[r][:, lo:hi], scalar1=inv[:], scalar2=None, op0=ALU.mult)
 
-        scores(0)
-        scores(1)
+        def norm_gpsimd(r, inv):
+            nc.gpsimd.tensor_scalar(out=y[:, r, :], in0=e_tiles[r][:], scalar1=inv[:], scalar2=0.0, op0=ALU.mult, op1=ALU.add)
+
+        for r in (0, 2, 1):
+            scores(r)
         weights(0)
-        scores(2)
-        weights(1)
-        norm_scalar(0, inverse(0), 0, N)
-        nc.sync.dma_start(out=out_rows[:, 0, :], in_=y[:, 0, :])
         scores(3)
+        weights(1)
+        norm_gpsimd(0, inverse(0))
+        nc.sync.dma_start(out=out_rows[:, 0, :], in_=y[:, 0, :])
         weights(2)
-        weights(3)
-        norm_vector(1, inverse(1), 0, N)
+        norm_gpsimd(1, inverse(1))
         nc.sync.dma_start(out=out_rows[:, 1, :], in_=y[:, 1, :])
+        weights(3)
         norm_vector(2, inverse(2), 0, N)
         nc.sync.dma_start(out=out_rows[:, 2, :], in_=y[:, 2, :])
         inv3 = inverse(3)
@@ -144,7 +153,8 @@ def tile_attend_plq_contrast_topk_kernel(tc, qT, k_words, k_scales, c_words, c_s
         y_bf = keep.tile([P, N, PACK], BF16, name="y_bf", align_bytes=64)
         dst = y_bf[:].rearrange("p (c i) r -> p c r i", i=4)
         src = y[:].rearrange("p r (c i) -> p c r i", i=4)
-        nc.vector.tensor_copy(out=dst[:, : V_COLS // 4], in_=src[:, : V_COLS // 4])
+        nc.vector.tensor_copy(out=dst[:, :64], in_=src[:, :64])
+        nc.vector.tensor_copy(out=dst[:, 64 : V_COLS // 4], in_=src[:, 64 : V_COLS // 4])
         nc.scalar.copy(out=dst[:, V_COLS // 4 :], in_=src[:, V_COLS // 4 :])
 
         y_codes = keep.tile([P, N], U32, name="y_codes", align_bytes=64)

from contextlib import ExitStack

import concourse.mybir as mybir

F32 = mybir.dt.float32
BF16 = mybir.dt.bfloat16
I32 = mybir.dt.int32
U32 = mybir.dt.uint32
U16 = mybir.dt.uint16
U8 = mybir.dt.uint8
FP8X4 = mybir.dt.float8_e4m3fn_x4
ALU = mybir.AluOpType
ACT = mybir.ActivationFunctionType
AX = mybir.AxisListType

P = 128
PACK = 4
T = 2048
N = 512
NQ = 512
D = 512
C_ROW = 8
V_COLS = 304
G_COLS = (0, 0, 512, 256)
Q_SPLIT = 96

FLOPS = 2 * 2 * NQ * N * D


def tile_attend_plq_contrast_topk_kernel(tc, qT, k_words, k_scales, c_words, c_scales, offs, out_0, out_1, out_2):
    nc = tc.nc
    with ExitStack() as ctx:
        keep = ctx.enter_context(tc.tile_pool(name="keep", bufs=1))
        psum = ctx.enter_context(tc.psum_pool(name="psum", bufs=1))

        offsets = keep.tile([P, N // 16], U16, name="offsets")
        q_raw = keep.tile([P, PACK, NQ], F32, name="q_raw")
        kw = keep.tile([P, T], I32, name="kw", align_bytes=64)
        cw = keep.tile([P, T], I32, name="cw", align_bytes=64)
        ks = keep.tile([P, T], U8, name="ks", align_bytes=64)
        cs = keep.tile([P, T], U8, name="cs", align_bytes=64)

        nc.vector.memset(cs[:].bitcast(I32), 0)
        nc.vector.memset(ks[:].bitcast(I32), 0)

        nc.sync.dma_start(out=q_raw[:], in_=qT[0].rearrange("(p j) q -> p j q", j=PACK))
        for r in range(4):
            nc.sync.dma_start(out=cs[C_ROW + r : P : 32, :].bitcast(I32), in_=c_scales[0, r:16:4, :].bitcast(I32))
        nc.sync.dma_start(offsets[:], offs)
        nc.sync.dma_start(out=cw[:], in_=c_words[0].rearrange("p t r -> p (t r)").bitcast(I32))
        for r in range(4):
            nc.sync.dma_start(out=ks[r:P:32, :].bitcast(I32), in_=k_scales[0, r:16:4, :].bitcast(I32))
        nc.sync.dma_start(out=kw[:], in_=k_words[0].rearrange("p t r -> p (t r)").bitcast(I32))

        csg = keep.tile([P, N], U8, name="csg", align_bytes=64)
        ksg = keep.tile([P, N], U8, name="ksg", align_bytes=64)
        cwg = keep.tile([P, N], U32, name="cwg", align_bytes=64)
        kwg = keep.tile([P, N], U32, name="kwg", align_bytes=64)

        nc.vector.tensor_copy(csg[:], cs[:].indirect(offsets[:]))

        q_bf = keep.tile([P, PACK, P, PACK], BF16, name="q_bf", align_bytes=64)
        q_dst = q_bf[:].rearrange("p r m j -> p m j r")
        q_src = q_raw[:].rearrange("p j (m r) -> p m j r", r=PACK)
        nc.scalar.activation(out=q_dst[:, :Q_SPLIT], in_=q_src[:, :Q_SPLIT], func=ACT.Copy)
        nc.vector.tensor_copy(out=q_dst[:, Q_SPLIT:], in_=q_src[:, Q_SPLIT:])
        q_codes = keep.tile([P, NQ], U32, name="q_codes", align_bytes=64)
        q_scales = keep.tile([P, NQ], U8, name="q_scales", align_bytes=64)
        nc.vector.quantize_mx(
            out=q_codes[:].bitcast(FP8X4), scales=q_scales[:], in_=q_bf[:].rearrange("p r m j -> p (r m j)")
        )

        nc.vector.tensor_copy(cwg[:], cw[:].bitcast(U32).indirect(offsets[:]))
        nc.vector.tensor_copy(ksg[:], ks[:].indirect(offsets[:]))

        z_sb = []
        for r in range(PACK):
            cols = slice(r * P, (r + 1) * P)
            z_ps = psum.tile([P, N], F32, name=f"z_ps{r}")
            nc.tensor.matmul_mx(
                out=z_ps[:], lhsT=q_codes[:, cols].bitcast(FP8X4), lhsT_scale=q_scales[:, cols],
                rhs=cwg[:].bitcast(FP8X4), rhs_scale=csg[C_ROW:P, :], start=True, stop=True,
            )
            half_z = keep.tile([P, N], F32, name=f"half_z{r}")
            nc.scalar.activation(out=half_z[:], in_=z_ps[:], func=ACT.Copy, scale=-0.5)
            z_sb.append(half_z)

        nc.vector.tensor_copy(kwg[:], kw[:].bitcast(U32).indirect(offsets[:]))

        y = keep.tile([P, PACK, N], F32, name="y")
        out_rows = out_0.rearrange("(p r) i -> p r i", r=PACK)
        g_tiles, e_tiles, sums = {}, [], []

        def scores(r):
            cols = slice(r * P, (r + 1) * P)
            a_ps = psum.tile([P, N], F32, name=f"a_ps{r}")
            nc.tensor.matmul_mx(
                out=a_ps[:], lhsT=q_codes[:, cols].bitcast(FP8X4), lhsT_scale=q_scales[:, cols],
                rhs=kwg[:].bitcast(FP8X4), rhs_scale=ksg[:], start=True, stop=True,
            )
            g = keep.tile([P, N], F32, name=f"g{r}")
            n_g = G_COLS[r]
            if n_g:
                a_sb = keep.tile([P, n_g], F32, name=f"a_sb{r}")
                nc.scalar.copy(out=a_sb[:], in_=a_ps[:, :n_g])
                nc.gpsimd.tensor_tensor(out=g[:, :n_g], in0=a_sb[:], in1=z_sb[r][:, :n_g], op=ALU.add)
            if n_g < N:
                nc.vector.tensor_tensor(out=g[:, n_g:], in0=a_ps[:, n_g:], in1=z_sb[r][:, n_g:], op=ALU.add)
            g_tiles[r] = g

        def weights(r):
            g = g_tiles[r]
            neg_max = keep.tile([P, 1], F32, name=f"neg_max{r}")
            nc.vector.tensor_reduce(out=neg_max[:], in_=g[:], axis=AX.X, op=ALU.max, negate=True)
            e = keep.tile([P, N], F32, name=f"e{r}")
            total = keep.tile([P, 1], F32, name=f"total{r}")
            nc.scalar.activation(out=e[:], in_=g[:], func=ACT.Exp, bias=neg_max[:], accum_out=total[:])
            e_tiles.append(e)
            sums.append(total)

        def inverse(r):
            inv = keep.tile([P, 1], F32, name=f"inv{r}")
            nc.vector.reciprocal(out=inv[:], in_=sums[r][:])
            return inv

        def norm_scalar(r, inv, lo, hi):
            nc.scalar.activation(out=y[:, r, lo:hi], in_=e_tiles[r][:, lo:hi], func=ACT.Copy, scale=inv[:])

        def norm_vector(r, inv, lo, hi):
            nc.vector.tensor_scalar(out=y[:, r, lo:hi], in0=e_tiles[r][:, lo:hi], scalar1=inv[:], scalar2=None, op0=ALU.mult)

        def norm_gpsimd(r, inv):
            nc.gpsimd.tensor_scalar(out=y[:, r, :], in0=e_tiles[r][:], scalar1=inv[:], scalar2=0.0, op0=ALU.mult, op1=ALU.add)

        for r in (0, 2, 1):
            scores(r)
        weights(0)
        scores(3)
        weights(1)
        norm_gpsimd(0, inverse(0))
        nc.sync.dma_start(out=out_rows[:, 0, :], in_=y[:, 0, :])
        weights(2)
        norm_gpsimd(1, inverse(1))
        nc.sync.dma_start(out=out_rows[:, 1, :], in_=y[:, 1, :])
        weights(3)
        norm_vector(2, inverse(2), 0, N)
        nc.sync.dma_start(out=out_rows[:, 2, :], in_=y[:, 2, :])
        inv3 = inverse(3)
        norm_vector(3, inv3, 0, V_COLS)
        norm_scalar(3, inv3, V_COLS, N)
        nc.sync.dma_start(out=out_rows[:, 3, :], in_=y[:, 3, :])

        y_bf = keep.tile([P, N, PACK], BF16, name="y_bf", align_bytes=64)
        dst = y_bf[:].rearrange("p (c i) r -> p c r i", i=4)
        src = y[:].rearrange("p r (c i) -> p c r i", i=4)
        nc.vector.tensor_copy(out=dst[:, :64], in_=src[:, :64])
        nc.vector.tensor_copy(out=dst[:, 64 : V_COLS // 4], in_=src[:, 64 : V_COLS // 4])
        nc.scalar.copy(out=dst[:, V_COLS // 4 :], in_=src[:, V_COLS // 4 :])

        y_codes = keep.tile([P, N], U32, name="y_codes", align_bytes=64)
        y_scales = keep.tile([P, N], U8, name="y_scales", align_bytes=64)
        words_out = out_1[0].rearrange("p i u -> p (i u)").bitcast(I32)
        flat = y_bf[:].rearrange("p i r -> p (i r)")
        for lo, hi in ((0, 256), (256, 512)):
            cols = slice(lo, hi)
            nc.vector.quantize_mx(
                out=y_codes[:, cols].bitcast(FP8X4), scales=y_scales[:, cols],
                in_=flat[:, PACK * lo : PACK * hi],
            )
            nc.sync.dma_start(out=words_out[:, cols], in_=y_codes[:, cols].bitcast(I32))
        for quad in range(4):
            queue = nc.scalar if quad % 2 else nc.sync
            queue.dma_start(
                out=out_2[0, 4 * quad : 4 * quad + 4, :].bitcast(I32),
                in_=y_scales[32 * quad : 32 * quad + 4, :].bitcast(I32),
            )
